import numpy as np
import ml_dtypes


def mxq(x, axis, fmt="e4m3"):
    dtype, down = {"e4m3": (ml_dtypes.float8_e4m3fn, 7), "e5m2": (ml_dtypes.float8_e5m2, 14)}[fmt]
    v = np.moveaxis(np.asarray(x, np.float32).astype(ml_dtypes.bfloat16).astype(np.float64), axis, -1)
    blocks = v.reshape(v.shape[:-1] + (-1, 32))
    amax = np.abs(blocks).max(-1, keepdims=True)
    byte = np.maximum(np.where(amax > 0, np.frexp(amax)[1] - 1 + 127, 0) - down, 1)
    scale = np.exp2(byte - 127.0)
    codes = (blocks / scale).astype(np.float32).astype(dtype).astype(np.float64)
    return np.moveaxis((codes * scale).reshape(v.shape), -1, axis)


WIDE = False


def mx_kscale(k):
    if not WIDE:
        return np.ones(k)
    levels = np.array([10, -10, 5, -5, 0])
    if k % 512:
        return np.exp2(np.random.permutation(np.resize(levels, k // 32))).repeat(32)
    a = np.empty((k // 512, 16))
    for p in range(k // 512):
        a[p, :8] = np.random.permutation(np.resize(levels, 8))
        for g in range(8):
            far = levels[np.abs(levels - a[p, g]) >= 10]
            a[p, g + 8] = far[np.random.randint(len(far))]
    return np.exp2(a.ravel()).repeat(32)


def f64(x):
    return np.asarray(x).astype(np.float64)


def striped(idx):
    return np.tile(idx.reshape(-1, 16).T, (8, 1)).astype(np.uint16)


def unstriped(offs):
    return offs[:16].T.reshape(-1).astype(np.int64)


def pack_weight(w):
    k, n = w.shape
    w = f64(np.asarray(w, np.float32).astype(ml_dtypes.bfloat16)).reshape(k // 32, 32, n)
    amax = np.abs(w).max(1)
    byte = np.clip(np.where(amax > 0, np.frexp(amax)[1] - 1 + 127 - 7, 1), 1, 254)
    scaled = (w * np.exp2(127.0 - byte)[:, None, :]).reshape(k, n).astype(np.float32)
    words = np.ascontiguousarray(scaled.reshape(k // 512, 128, 4, n).transpose(0, 1, 3, 2)).astype(ml_dtypes.float8_e4m3fn).view(np.uint8)
    return words, np.ascontiguousarray(byte.astype(np.uint8).reshape(k // 512, 16, n))


def unpack_weight(words, scales):
    g, p, n, _ = words.shape
    vals = np.ascontiguousarray(words).view(ml_dtypes.float8_e4m3fn).astype(np.float64) * np.repeat(np.exp2(scales.astype(np.float64) - 127.0), 8, axis=1)[..., None]
    return vals.transpose(0, 1, 3, 2).reshape(g * 512, n)


E2M1 = np.array([0.0, 0.5, 1.0, 1.5, 2.0, 3.0, 4.0, 6.0, -0.0, -0.5, -1.0, -1.5, -2.0, -3.0, -4.0, -6.0])


def pack_fp4(w):
    k, n = w.shape
    w = f64(np.asarray(w, np.float32).astype(ml_dtypes.bfloat16)).reshape(k // 32, 32, n)
    amax = np.abs(w).max(1)
    mant, ex = np.frexp(amax / 6.0)
    byte = np.clip(np.where(amax > 0, np.where(mant > 0.5, ex, ex - 1) + 127, 1), 1, 254)
    scaled = (w * np.exp2(127.0 - byte)[:, None, :]).reshape(k, n).astype(np.float32)
    c = np.ascontiguousarray(scaled.reshape(k // 512, 128, 4, n).transpose(0, 1, 3, 2)).astype(ml_dtypes.float4_e2m1fn).view(np.uint8) & 0xF
    words = (c[..., 0::2] | (c[..., 1::2] << 4)).reshape(k // 512, 128, 2 * n)
    return np.ascontiguousarray(words), np.ascontiguousarray(byte.astype(np.uint8).reshape(k // 512, 16, n))


def unpack_fp4(words, scales):
    g, _, n = scales.shape
    words = np.ascontiguousarray(words).reshape(g, 128, n, 2)
    nib = np.empty((g, 128, n, 4), np.uint8)
    nib[..., 0::2] = words & 0xF
    nib[..., 1::2] = words >> 4
    vals = E2M1[nib] * np.repeat(np.exp2(scales.astype(np.float64) - 127.0), 8, axis=1)[..., None]
    return vals.transpose(0, 1, 3, 2).reshape(g * 512, n)


def sigmoid(v):
    return 1.0 / (1.0 + np.exp(-np.maximum(v, -700.0)))

def planes(y):
    n, m = y.shape
    v = y.astype(np.float32).astype(ml_dtypes.bfloat16).astype(np.float64).reshape(n // 32, 32, m)
    top = np.abs(v).max(1)
    byte = np.clip(np.where(top > 0, np.frexp(top)[1] - 1 + 127 - 7, 1), 1, 254)
    codes = (v * np.exp2(127.0 - byte)[:, None, :]).reshape(n, m).astype(np.float32).astype(ml_dtypes.float8_e4m3fn).view(np.uint8)
    words = codes.reshape(n // 512, 128, 4, m).transpose(0, 1, 3, 2)
    return np.ascontiguousarray(words), np.ascontiguousarray(byte.astype(np.uint8).reshape(n // 512, 16, m))


K, T, S, V, N, H = 512, 2048, 512, 512, 512, 512


def setup_inputs():
    n = np.random.standard_normal
    s = mx_kscale(K)[:, None]
    u = mx_kscale(S)
    packed_xT = pack_weight(n((K, T)) * s)
    packed_w1 = pack_fp4(n((K, H)) / np.sqrt(K) / s)
    packed_w2 = pack_fp4(n((V, N)) / np.sqrt(V) / u[:, None])
    return {
        "x_words": packed_xT[0],
        "x_scales": packed_xT[1],
        "w1_words": packed_w1[0],
        "w1_scales": packed_w1[1],
        "gs": (np.random.uniform(0.5, 1.5, (K, 1)) / s).astype(np.float32),
        "gt": (np.random.uniform(0.5, 1.5, (V, 1)) * u[:, None]).astype(np.float32),
        "w2_words": packed_w2[0],
        "w2_scales": packed_w2[1],
        "offs": striped(np.random.permutation(T)[:S]),
        "cand": striped(np.random.permutation(T)[:V]),
    }


def reference(x_words, x_scales, w1_words, w1_scales, gs, gt, w2_words, w2_scales, offs, cand):
    x_cand = unpack_weight(x_words, x_scales)[:, unstriped(cand)]
    xq = unpack_weight(x_words, x_scales)[:, unstriped(offs)]
    h = unpack_fp4(w1_words, w1_scales).T @ xq
    z = f64(gs) * h
    s = 0.0625 * ((x_cand.T @ mxq(z, 0, "e4m3")))
    z2 = f64(gt) * sigmoid(s)
    out_0 = unpack_fp4(w2_words, w2_scales).T @ mxq(z2, 0, "e4m3")
    return (out_0,) + planes(out_0)

@@ -1,0 +1,279 @@
+from contextlib import ExitStack
+
+import concourse.mybir as mybir
+
+K, T, S, V, N, H = 512, 2048, 512, 512, 512, 512
+FLOPS = 2 * K * H * S + 2 * K * V * S + 2 * V * N * S
+
+F32 = mybir.dt.float32
+BF16 = mybir.dt.bfloat16
+I32 = mybir.dt.int32
+U32 = mybir.dt.uint32
+U16 = mybir.dt.uint16
+U8 = mybir.dt.uint8
+FP8X4 = mybir.dt.float8_e4m3fn_x4
+FP4X4 = mybir.dt.float4_e2m1fn_x4
+MULT = mybir.AluOpType.mult
+ACT = mybir.ActivationFunctionType
+
+P = 128
+C = 128
+NC = S // C
+HALF = 256
+
+
+def tile_picked_candread_sigmoid_po_kernel(
+    tc, x_words, x_scales, w1_words, w1_scales, gs, gt, w2_words, w2_scales, offs, cand, out_0, out_1, out_2
+):
+    nc = tc.nc
+    with ExitStack() as ctx:
+        keep = ctx.enter_context(tc.tile_pool(name="keep", bufs=1))
+        psum = ctx.enter_context(tc.psum_pool(name="psum", bufs=1))
+
+        def kt(shape, dt, name):
+            return keep.tile(shape, dt, name=name, align_bytes=64)
+
+        offs_t = kt([P, S // 16], U16, "offs_t")
+        cand_t = kt([P, V // 16], U16, "cand_t")
+        xw = kt([P, T], I32, "xw")
+        xs = kt([P, T], U8, "xs")
+        w1w_raw = kt([P, 2 * H], U8, "w1w_raw")
+        w2w_raw = w1w_raw
+        w1s_raw = kt([P, H], U8, "w1s_raw")
+        w2s_raw = w1s_raw
+        w1w = kt([P, 2 * H], U8, "w1w")
+        w2w = kt([P, 2 * N], U8, "w2w")
+        w1s = kt([P, H], U8, "w1s")
+        w2s = kt([P, N], U8, "w2s")
+        gs_t = kt([P, 4], F32, "gs_t")
+        gt_t = kt([P, 4], F32, "gt_t")
+        qw = [kt([P, HALF], I32, "qw")] * 2
+        qs = [kt([P, HALF], U8, "qs")] * 2
+        cw = kt([P, V], I32, "cw")
+        cw_raw = kt([P, V], I32, "cw_raw")
+        cs_raw = kt([P, V], U8, "cs_raw")
+        cs = kt([P, V], U8, "cs")
+        ow = kt([P, S], I32, "ow")
+        osc = kt([P, S], U8, "osc")
+
+        def load_scales(engs, dst, src):
+            for q in range(4):
+                engs[q].dma_start(out=dst[32 * q : 32 * q + 4, :].bitcast(I32), in_=src[0, 4 * q : 4 * q + 4, :].bitcast(I32))
+
+        def deal_words(eng, dst, src):
+            eng.tensor_copy(
+                out=dst[:].rearrange("p (t m b) -> p t m b", t=4, b=2),
+                in_=src[:].rearrange("p (m t b) -> p t m b", t=4, b=2),
+            )
+
+        def deal_bytes(eng, dst, src):
+            eng.tensor_copy(
+                out=dst[:].rearrange("p (t m) -> p t m", t=4),
+                in_=src[:].rearrange("p (m t) -> p t m", t=4),
+            )
+
+        nc.vector.memset(xs[:].bitcast(I32), 0)
+        nc.vector.memset(w1s_raw[:].bitcast(I32), 0)
+        two = [nc.sync, nc.scalar, nc.sync, nc.scalar]
+        nc.sync.dma_start(offs_t[:], offs)
+        load_scales(two, xs, x_scales)
+        nc.scalar.dma_start(out=w1w_raw[:].bitcast(I32), in_=w1_words[0].bitcast(I32))
+        nc.sync.dma_start(cand_t[:], cand)
+        nc.scalar.dma_start(out=xw[:], in_=x_words[0].rearrange("p n t -> p (n t)").bitcast(I32))
+        load_scales(two, w1s_raw, w1_scales)
+        nc.sync.dma_start(out=gs_t[:], in_=gs.rearrange("(p t) o -> p (t o)", t=4))
+        nc.sync.dma_start(out=gt_t[:], in_=gt.rearrange("(p t) o -> p (t o)", t=4))
+
+        out0_v = out_0.rearrange("(p t) n -> p t n", t=4)
+        out1_v = out_1[0].rearrange("p n t -> p (n t)").bitcast(I32)
+
+        def gather_qs(h):
+            nc.vector.tensor_copy(out=qs[h][:], in_=xs[:].indirect(offs_t[:, 16 * h : 16 * h + 16]))
+
+        def gather_qw(h):
+            nc.vector.tensor_copy(out=qw[h][:].bitcast(U32), in_=xw[:].bitcast(U32).indirect(offs_t[:, 16 * h : 16 * h + 16]))
+
+        def gather_cs():
+            nc.vector.tensor_copy(out=cs_raw[:], in_=xs[:].indirect(cand_t[:]))
+            deal_bytes(nc.vector, cs, cs_raw)
+
+        def gather_cw():
+            nc.vector.tensor_copy(
+                out=cw[:].bitcast(U32).rearrange("p (t m) -> p m t", t=4), in_=xw[:].bitcast(U32).indirect(cand_t[:])
+            )
+
+        def gather_cw2():
+            nc.vector.tensor_copy(out=cw_raw[:].bitcast(U32), in_=xw[:].bitcast(U32).indirect(cand_t[:]))
+            nc.vector.tensor_copy(
+                out=cw[:].rearrange("p (t m) -> p t m", t=4), in_=cw_raw[:].rearrange("p (m t) -> p t m", t=4)
+            )
+
+        def product(bank, lw, ls, ldt, lbytes, rw, rs, width):
+            for t in range(4):
+                nc.tensor.matmul_mx(
+                    out=bank(t),
+                    lhsT=lw[:, lbytes * t : lbytes * (t + 1)].bitcast(ldt),
+                    lhsT_scale=ls[:, P * t : P * (t + 1)],
+                    rhs=rw.bitcast(FP8X4),
+                    rhs_scale=rs,
+                    start=True,
+                    stop=True,
+                )
+
+        st = {}
+
+        def load_w2():
+            nc.sync.dma_start(out=w2w_raw[:].bitcast(I32), in_=w2_words[0].bitcast(I32))
+            load_scales([nc.sync] * 4, w2s_raw, w2_scales)
+
+        def mm1(c):
+            h, o = divmod(c * C, HALF)
+            b = psum.tile([P, 4, C], F32, name="b1_%d" % c, tag="b1", bufs=2)
+            product(lambda t: b[:, t, :], w1w, w1s, FP4X4, 2 * P, qw[h][:, o : o + C], qs[h][:, o : o + C], C)
+            st["b1", c] = b
+
+        def scale1(c):
+            zb = kt([P, C, 4], BF16, "zb%d" % c)
+            nc.vector.tensor_tensor(
+                out=zb[:], in0=st["b1", c][:].rearrange("p t n -> p n t"),
+                in1=gs_t[:].unsqueeze(1).to_broadcast([P, C, 4]), op=MULT,
+            )
+            st["zb", c] = zb[:].rearrange("p n t -> p (n t)")
+
+        def scale1_s(c):
+            zp = kt([P, 4, C], BF16, "zp%d" % c)
+            for t in range(4):
+                nc.scalar.activation(out=zp[:, t, :], in_=st["b1", c][:, t, :], func=ACT.Copy, scale=gs_t[:, t : t + 1])
+            st["zp", c] = zp
+
+        def weave1(c):
+            zb = kt([P, C, 4], BF16, "zb%d" % c)
+            nc.vector.tensor_copy(
+                out=zb[:].rearrange("p (c i) t -> p c t i", i=4), in_=st["zp", c][:].rearrange("p t (c i) -> p c t i", i=4)
+            )
+            st["zb", c] = zb[:].rearrange("p n t -> p (n t)")
+
+        def quant(key, c):
+            w = kt([P, C], I32, "%sw%d" % (key, c))
+            s = kt([P, C], U8, "%ss%d" % (key, c))
+            nc.vector.quantize_mx(out=w[:].bitcast(FP8X4), scales=s[:], in_=st[key, c])
+            st[key + "q", c] = (w, s)
+
+        def mm2(c):
+            w, s = st["zbq", c]
+            b = psum.tile([P, 4, C], F32, name="b2_%d" % c, tag="b2", bufs=3)
+            product(lambda t: b[:, t, :], cw, cs, FP8X4, P, w[:], s[:], C)
+            st["b2", c] = b
+
+        def sigm(c):
+            sg = kt([P, C, 4], F32, "sg%d" % c)
+            nc.scalar.activation(out=sg[:], in_=st["b2", c][:].rearrange("p t n -> p n t"), func=ACT.Sigmoid, scale=0.0625)
+            st["sg", c] = sg
+
+        def scale2(c, eng=nc.vector):
+            yb = kt([P, C, 4], BF16, "yb%d" % c)
+            eng.tensor_tensor(
+                out=yb[:], in0=st["sg", c][:], in1=gt_t[:].unsqueeze(1).to_broadcast([P, C, 4]), op=MULT,
+            )
+            st["yb", c] = yb[:].rearrange("p n t -> p (n t)")
+
+        def mm3(c):
+            w, s = st["ybq", c]
+            b = psum.tile([P, 4, C], F32, name="b3_%d" % c, tag="b3", bufs=3)
+            product(lambda t: b[:, t, :], w2w, w2s, FP4X4, 2 * P, w[:], s[:], C)
+            st["b3", c] = b
+
+        def evac3(c, vec=False):
+            of = kt([P, 4, C], F32, "of%d" % c)
+            if vec:
+                nc.vector.tensor_copy(out=of[:], in_=st["b3", c][:])
+            else:
+                nc.scalar.copy(out=of[:], in_=st["b3", c][:])
+            st["of", c] = of
+
+        def store0(c, eng=nc.sync):
+            eng.dma_start(out=out0_v[:, :, c * C : (c + 1) * C], in_=st["of", c][:])
+
+        def weave3(c, vec=False):
+            ob = kt([P, C, 4], BF16, "ob%d" % c)
+            if vec:
+                nc.vector.tensor_copy(
+                    out=ob[:].rearrange("p (c i) t -> p c t i", i=4), in_=st["of", c][:].rearrange("p t (c i) -> p c t i", i=4)
+                )
+            else:
+                nc.scalar.copy(out=ob[:], in_=st["b3", c][:].rearrange("p t n -> p n t"))
+            st["ob", c] = ob[:].rearrange("p n t -> p (n t)")
+
+        def quant3(c):
+            nc.vector.quantize_mx(out=ow[:, c * C : (c + 1) * C].bitcast(FP8X4), scales=osc[:, c * C : (c + 1) * C], in_=st["ob", c])
+
+        def store1(a, b, eng=nc.sync):
+            eng.dma_start(out=out1_v[:, a * C : b * C], in_=ow[:, a * C : b * C])
+
+        def store2(engs):
+            for q in range(4):
+                engs[q].dma_start(out=out_2[0, 4 * q : 4 * q + 4, :].bitcast(I32), in_=osc[32 * q : 32 * q + 4, :].bitcast(I32))
+
+        gather_qs(0)
+        deal_words(nc.vector, w1w, w1w_raw)
+        gather_cs()
+        deal_bytes(nc.vector, w1s, w1s_raw)
+        load_w2()
+        gather_qw(0)
+        mm1(0)
+        mm1(1)
+        gather_cw()
+        scale1(0)
+        scale1_s(1)
+        gather_qs(1)
+        quant("zb", 0)
+        mm2(0)
+        sigm(0)
+        weave1(1)
+        gather_qw(1)
+        quant("zb", 1)
+        mm2(1)
+        mm1(2)
+        mm1(3)
+        sigm(1)
+        deal_words(nc.vector, w2w, w2w_raw)
+        deal_bytes(nc.vector, w2s, w2s_raw)
+        scale2(0)
+        scale1(2)
+        quant("yb", 0)
+        mm3(0)
+        quant("zb", 2)
+        mm2(2)
+        scale1(3)
+        sigm(2)
+        evac3(0)
+        store0(0)
+        weave3(0)
+        scale2(1)
+        quant("zb", 3)
+        mm2(3)
+        quant("yb", 1)
+        mm3(1)
+        sigm(3)
+        evac3(1)
+        store0(1)
+        weave3(1)
+        scale2(2)
+        quant3(0)
+        quant("yb", 2)
+        mm3(2)
+        scale2(3)
+        quant3(1)
+        store1(0, 2)
+        quant("yb", 3)
+        mm3(3)
+        weave3(2)
+        evac3(2)
+        store0(2)
+        evac3(3)
+        store0(3)
+        quant3(2)
+        weave3(3, True)
+        quant3(3)
+        store1(2, 4)
+        store2([nc.sync, nc.sync, nc.scalar, nc.scalar])

@@ -38,17 +38,18 @@ def tile_picked_candread_sigmoid_po_kernel(
         xw = kt([P, T], I32, "xw")
         xs = kt([P, T], U8, "xs")
         w1w_raw = kt([P, 2 * H], U8, "w1w_raw")
-        w2w_raw = w1w_raw
+        w2w_raw = kt([P, 2 * N], U8, "w2w_raw")
         w1s_raw = kt([P, H], U8, "w1s_raw")
-        w2s_raw = w1s_raw
+        w2s_raw = kt([P, N], U8, "w2s_raw")
         w1w = kt([P, 2 * H], U8, "w1w")
         w2w = kt([P, 2 * N], U8, "w2w")
         w1s = kt([P, H], U8, "w1s")
         w2s = kt([P, N], U8, "w2s")
         gs_t = kt([P, 4], F32, "gs_t")
         gt_t = kt([P, 4], F32, "gt_t")
-        qw = [kt([P, HALF], I32, "qw")] * 2
-        qs = [kt([P, HALF], U8, "qs")] * 2
+        qw = [kt([P, HALF], I32, "qw%d" % h) for h in range(2)]
+        qs_all = kt([P, S], U8, "qs_all")
+        qs = [qs_all[:, 0:HALF], qs_all[:, HALF:S]]
         cw = kt([P, V], I32, "cw")
         cw_raw = kt([P, V], I32, "cw_raw")
         cs_raw = kt([P, V], U8, "cs_raw")
@@ -74,15 +75,17 @@ def tile_picked_candread_sigmoid_po_kernel(
 
         nc.vector.memset(xs[:].bitcast(I32), 0)
         nc.vector.memset(w1s_raw[:].bitcast(I32), 0)
-        two = [nc.sync, nc.scalar, nc.sync, nc.scalar]
+        nc.vector.memset(w2s_raw[:].bitcast(I32), 0)
         nc.sync.dma_start(offs_t[:], offs)
-        load_scales(two, xs, x_scales)
         nc.scalar.dma_start(out=w1w_raw[:].bitcast(I32), in_=w1_words[0].bitcast(I32))
-        nc.sync.dma_start(cand_t[:], cand)
+        load_scales([nc.sync, nc.scalar, nc.sync, nc.scalar], xs, x_scales)
         nc.scalar.dma_start(out=xw[:], in_=x_words[0].rearrange("p n t -> p (n t)").bitcast(I32))
-        load_scales(two, w1s_raw, w1_scales)
+        load_scales([nc.sync] * 4, w1s_raw, w1_scales)
         nc.sync.dma_start(out=gs_t[:], in_=gs.rearrange("(p t) o -> p (t o)", t=4))
         nc.sync.dma_start(out=gt_t[:], in_=gt.rearrange("(p t) o -> p (t o)", t=4))
+        nc.sync.dma_start(cand_t[:], cand)
+        nc.sync.dma_start(out=w2w_raw[:].bitcast(I32), in_=w2_words[0].bitcast(I32))
+        load_scales([nc.sync] * 4, w2s_raw, w2_scales)
 
         out0_v = out_0.rearrange("(p t) n -> p t n", t=4)
         out1_v = out_1[0].rearrange("p n t -> p (n t)").bitcast(I32)
@@ -122,13 +125,21 @@ def tile_picked_candread_sigmoid_po_kernel(
 
         st = {}
 
-        def load_w2():
-            nc.sync.dma_start(out=w2w_raw[:].bitcast(I32), in_=w2_words[0].bitcast(I32))
-            load_scales([nc.sync] * 4, w2s_raw, w2_scales)
+        def gather_qs_all():
+            nc.vector.tensor_copy(out=qs_all[:], in_=xs[:].indirect(offs_t[:]))
+
+        def mm1h(h):
+            bs = [psum.tile([P, 2, HALF], F32, name="h%d_%d" % (h, u), tag="bank", bufs=8) for u in range(2)]
+            zp = kt([P, 4, HALF], BF16, "zph%d" % h)
+            product(lambda t: bs[t // 2][:, t % 2, :], w1w, w1s, FP4X4, 2 * P, qw[h][:], qs[h], HALF)
+            for t in range(4):
+                nc.scalar.activation(out=zp[:, t, :], in_=bs[t // 2][:, t % 2, :], func=ACT.Copy, scale=gs_t[:, t : t + 1])
+            for j in range(2):
+                st["zp", 2 * h + j] = zp[:, :, j * C : (j + 1) * C]
 
         def mm1(c):
             h, o = divmod(c * C, HALF)
-            b = psum.tile([P, 4, C], F32, name="b1_%d" % c, tag="b1", bufs=2)
+            b = psum.tile([P, 4, C], F32, name="b1_%d" % c, tag="bank", bufs=8)
             product(lambda t: b[:, t, :], w1w, w1s, FP4X4, 2 * P, qw[h][:, o : o + C], qs[h][:, o : o + C], C)
             st["b1", c] = b
 
@@ -149,7 +160,7 @@ def tile_picked_candread_sigmoid_po_kernel(
         def weave1(c):
             zb = kt([P, C, 4], BF16, "zb%d" % c)
             nc.vector.tensor_copy(
-                out=zb[:].rearrange("p (c i) t -> p c t i", i=4), in_=st["zp", c][:].rearrange("p t (c i) -> p c t i", i=4)
+                out=zb[:].rearrange("p (c i) t -> p c t i", i=4), in_=st["zp", c].rearrange("p t (c i) -> p c t i", i=4)
             )
             st["zb", c] = zb[:].rearrange("p n t -> p (n t)")
 
@@ -161,7 +172,7 @@ def tile_picked_candread_sigmoid_po_kernel(
 
         def mm2(c):
             w, s = st["zbq", c]
-            b = psum.tile([P, 4, C], F32, name="b2_%d" % c, tag="b2", bufs=3)
+            b = psum.tile([P, 4, C], F32, name="b2_%d" % c, tag="bank", bufs=8)
             product(lambda t: b[:, t, :], cw, cs, FP8X4, P, w[:], s[:], C)
             st["b2", c] = b
 
@@ -179,7 +190,7 @@ def tile_picked_candread_sigmoid_po_kernel(
 
         def mm3(c):
             w, s = st["ybq", c]
-            b = psum.tile([P, 4, C], F32, name="b3_%d" % c, tag="b3", bufs=3)
+            b = psum.tile([P, 4, C], F32, name="b3_%d" % c, tag="bank", bufs=8)
             product(lambda t: b[:, t, :], w2w, w2s, FP4X4, 2 * P, w[:], s[:], C)
             st["b3", c] = b
 
@@ -214,66 +225,61 @@ def tile_picked_candread_sigmoid_po_kernel(
             for q in range(4):
                 engs[q].dma_start(out=out_2[0, 4 * q : 4 * q + 4, :].bitcast(I32), in_=osc[32 * q : 32 * q + 4, :].bitcast(I32))
 
-        gather_qs(0)
         deal_words(nc.vector, w1w, w1w_raw)
-        gather_cs()
+        gather_qs_all()
         deal_bytes(nc.vector, w1s, w1s_raw)
-        load_w2()
         gather_qw(0)
-        mm1(0)
-        mm1(1)
+        mm1h(0)
+        gather_qw(1)
+        mm1h(1)
+        gather_cs()
         gather_cw()
-        scale1(0)
-        scale1_s(1)
-        gather_qs(1)
+        weave1(0)
+        weave1(1)
         quant("zb", 0)
         mm2(0)
         sigm(0)
-        weave1(1)
-        gather_qw(1)
         quant("zb", 1)
         mm2(1)
-        mm1(2)
-        mm1(3)
         sigm(1)
+        weave1(2)
+        weave1(3)
+        quant("zb", 2)
+        mm2(2)
+        sigm(2)
+        quant("zb", 3)
+        mm2(3)
+        sigm(3)
         deal_words(nc.vector, w2w, w2w_raw)
         deal_bytes(nc.vector, w2s, w2s_raw)
         scale2(0)
-        scale1(2)
+        scale2(1)
         quant("yb", 0)
         mm3(0)
-        quant("zb", 2)
-        mm2(2)
-        scale1(3)
-        sigm(2)
         evac3(0)
         store0(0)
-        weave3(0)
-        scale2(1)
-        quant("zb", 3)
-        mm2(3)
+        scale2(2)
         quant("yb", 1)
         mm3(1)
-        sigm(3)
         evac3(1)
         store0(1)
-        weave3(1)
-        scale2(2)
-        quant3(0)
+        scale2(3)
         quant("yb", 2)
         mm3(2)
-        scale2(3)
-        quant3(1)
-        store1(0, 2)
-        quant("yb", 3)
-        mm3(3)
-        weave3(2)
         evac3(2)
         store0(2)
+        quant("yb", 3)
+        mm3(3)
         evac3(3)
         store0(3)
+        weave3(0, True)
+        weave3(1, True)
+        quant3(0)
+        quant3(1)
+        store1(0, 2)
+        weave3(2, True)
         quant3(2)
         weave3(3, True)
         quant3(3)
         store1(2, 4)
-        store2([nc.sync, nc.sync, nc.scalar, nc.scalar])
+        store2([nc.sync, nc.scalar, nc.scalar, nc.scalar])

from contextlib import ExitStack

import concourse.mybir as mybir

K, T, S, V, N, H = 512, 2048, 512, 512, 512, 512
FLOPS = 2 * K * H * S + 2 * K * V * S + 2 * V * N * S

F32 = mybir.dt.float32
BF16 = mybir.dt.bfloat16
I32 = mybir.dt.int32
U32 = mybir.dt.uint32
U16 = mybir.dt.uint16
U8 = mybir.dt.uint8
FP8X4 = mybir.dt.float8_e4m3fn_x4
FP4X4 = mybir.dt.float4_e2m1fn_x4
MULT = mybir.AluOpType.mult
ACT = mybir.ActivationFunctionType

P = 128
C = 128
NC = S // C
HALF = 256


def tile_picked_candread_sigmoid_po_kernel(
    tc, x_words, x_scales, w1_words, w1_scales, gs, gt, w2_words, w2_scales, offs, cand, out_0, out_1, out_2
):
    nc = tc.nc
    with ExitStack() as ctx:
        keep = ctx.enter_context(tc.tile_pool(name="keep", bufs=1))
        psum = ctx.enter_context(tc.psum_pool(name="psum", bufs=1))

        def kt(shape, dt, name):
            return keep.tile(shape, dt, name=name, align_bytes=64)

        offs_t = kt([P, S // 16], U16, "offs_t")
        cand_t = kt([P, V // 16], U16, "cand_t")
        xw = kt([P, T], I32, "xw")
        xs = kt([P, T], U8, "xs")
        w1w_raw = kt([P, 2 * H], U8, "w1w_raw")
        w2w_raw = kt([P, 2 * N], U8, "w2w_raw")
        w1s_raw = kt([P, H], U8, "w1s_raw")
        w2s_raw = kt([P, N], U8, "w2s_raw")
        w1w = kt([P, 2 * H], U8, "w1w")
        w2w = kt([P, 2 * N], U8, "w2w")
        w1s = kt([P, H], U8, "w1s")
        w2s = kt([P, N], U8, "w2s")
        gs_t = kt([P, 4], F32, "gs_t")
        gt_t = kt([P, 4], F32, "gt_t")
        qw = [kt([P, HALF], I32, "qw%d" % h) for h in range(2)]
        qs_all = kt([P, S], U8, "qs_all")
        qs = [qs_all[:, 0:HALF], qs_all[:, HALF:S]]
        cw = kt([P, V], I32, "cw")
        cw_raw = kt([P, V], I32, "cw_raw")
        cs_raw = kt([P, V], U8, "cs_raw")
        cs = kt([P, V], U8, "cs")
        ow = kt([P, S], I32, "ow")
        osc = kt([P, S], U8, "osc")

        def load_scales(engs, dst, src):
            for q in range(4):
                engs[q].dma_start(out=dst[32 * q : 32 * q + 4, :].bitcast(I32), in_=src[0, 4 * q : 4 * q + 4, :].bitcast(I32))

        def deal_words(eng, dst, src):
            eng.tensor_copy(
                out=dst[:].rearrange("p (t m b) -> p t m b", t=4, b=2),
                in_=src[:].rearrange("p (m t b) -> p t m b", t=4, b=2),
            )

        def deal_bytes(eng, dst, src):
            eng.tensor_copy(
                out=dst[:].rearrange("p (t m) -> p t m", t=4),
                in_=src[:].rearrange("p (m t) -> p t m", t=4),
            )

        nc.vector.memset(xs[:].bitcast(I32), 0)
        nc.vector.memset(w1s_raw[:].bitcast(I32), 0)
        nc.vector.memset(w2s_raw[:].bitcast(I32), 0)
        nc.sync.dma_start(offs_t[:], offs)
        nc.scalar.dma_start(out=w1w_raw[:].bitcast(I32), in_=w1_words[0].bitcast(I32))
        load_scales([nc.sync, nc.scalar, nc.sync, nc.scalar], xs, x_scales)
        nc.scalar.dma_start(out=xw[:], in_=x_words[0].rearrange("p n t -> p (n t)").bitcast(I32))
        load_scales([nc.sync] * 4, w1s_raw, w1_scales)
        nc.sync.dma_start(out=gs_t[:], in_=gs.rearrange("(p t) o -> p (t o)", t=4))
        nc.sync.dma_start(out=gt_t[:], in_=gt.rearrange("(p t) o -> p (t o)", t=4))
        nc.sync.dma_start(cand_t[:], cand)
        nc.sync.dma_start(out=w2w_raw[:].bitcast(I32), in_=w2_words[0].bitcast(I32))
        load_scales([nc.sync] * 4, w2s_raw, w2_scales)

        out0_v = out_0.rearrange("(p t) n -> p t n", t=4)
        out1_v = out_1[0].rearrange("p n t -> p (n t)").bitcast(I32)

        def gather_qs(h):
            nc.vector.tensor_copy(out=qs[h][:], in_=xs[:].indirect(offs_t[:, 16 * h : 16 * h + 16]))

        def gather_qw(h):
            nc.vector.tensor_copy(out=qw[h][:].bitcast(U32), in_=xw[:].bitcast(U32).indirect(offs_t[:, 16 * h : 16 * h + 16]))

        def gather_cs():
            nc.vector.tensor_copy(out=cs_raw[:], in_=xs[:].indirect(cand_t[:]))
            deal_bytes(nc.vector, cs, cs_raw)

        def gather_cw():
            nc.vector.tensor_copy(
                out=cw[:].bitcast(U32).rearrange("p (t m) -> p m t", t=4), in_=xw[:].bitcast(U32).indirect(cand_t[:])
            )

        def gather_cw2():
            nc.vector.tensor_copy(out=cw_raw[:].bitcast(U32), in_=xw[:].bitcast(U32).indirect(cand_t[:]))
            nc.vector.tensor_copy(
                out=cw[:].rearrange("p (t m) -> p t m", t=4), in_=cw_raw[:].rearrange("p (m t) -> p t m", t=4)
            )

        def product(bank, lw, ls, ldt, lbytes, rw, rs, width):
            for t in range(4):
                nc.tensor.matmul_mx(
                    out=bank(t),
                    lhsT=lw[:, lbytes * t : lbytes * (t + 1)].bitcast(ldt),
                    lhsT_scale=ls[:, P * t : P * (t + 1)],
                    rhs=rw.bitcast(FP8X4),
                    rhs_scale=rs,
                    start=True,
                    stop=True,
                )

        st = {}

        def gather_qs_all():
            nc.vector.tensor_copy(out=qs_all[:], in_=xs[:].indirect(offs_t[:]))

        def mm1h(h):
            bs = [psum.tile([P, 2, HALF], F32, name="h%d_%d" % (h, u), tag="bank", bufs=8) for u in range(2)]
            zp = kt([P, 4, HALF], BF16, "zph%d" % h)
            product(lambda t: bs[t // 2][:, t % 2, :], w1w, w1s, FP4X4, 2 * P, qw[h][:], qs[h], HALF)
            for t in range(4):
                nc.scalar.activation(out=zp[:, t, :], in_=bs[t // 2][:, t % 2, :], func=ACT.Copy, scale=gs_t[:, t : t + 1])
            for j in range(2):
                st["zp", 2 * h + j] = zp[:, :, j * C : (j + 1) * C]

        def mm1(c):
            h, o = divmod(c * C, HALF)
            b = psum.tile([P, 4, C], F32, name="b1_%d" % c, tag="bank", bufs=8)
            product(lambda t: b[:, t, :], w1w, w1s, FP4X4, 2 * P, qw[h][:, o : o + C], qs[h][:, o : o + C], C)
            st["b1", c] = b

        def scale1(c):
            zb = kt([P, C, 4], BF16, "zb%d" % c)
            nc.vector.tensor_tensor(
                out=zb[:], in0=st["b1", c][:].rearrange("p t n -> p n t"),
                in1=gs_t[:].unsqueeze(1).to_broadcast([P, C, 4]), op=MULT,
            )
            st["zb", c] = zb[:].rearrange("p n t -> p (n t)")

        def scale1_s(c):
            zp = kt([P, 4, C], BF16, "zp%d" % c)
            for t in range(4):
                nc.scalar.activation(out=zp[:, t, :], in_=st["b1", c][:, t, :], func=ACT.Copy, scale=gs_t[:, t : t + 1])
            st["zp", c] = zp

        def weave1(c):
            zb = kt([P, C, 4], BF16, "zb%d" % c)
            nc.vector.tensor_copy(
                out=zb[:].rearrange("p (c i) t -> p c t i", i=4), in_=st["zp", c].rearrange("p t (c i) -> p c t i", i=4)
            )
            st["zb", c] = zb[:].rearrange("p n t -> p (n t)")

        def quant(key, c):
            w = kt([P, C], I32, "%sw%d" % (key, c))
            s = kt([P, C], U8, "%ss%d" % (key, c))
            nc.vector.quantize_mx(out=w[:].bitcast(FP8X4), scales=s[:], in_=st[key, c])
            st[key + "q", c] = (w, s)

        def mm2(c):
            w, s = st["zbq", c]
            b = psum.tile([P, 4, C], F32, name="b2_%d" % c, tag="bank", bufs=8)
            product(lambda t: b[:, t, :], cw, cs, FP8X4, P, w[:], s[:], C)
            st["b2", c] = b

        def sigm(c):
            sg = kt([P, C, 4], F32, "sg%d" % c)
            nc.scalar.activation(out=sg[:], in_=st["b2", c][:].rearrange("p t n -> p n t"), func=ACT.Sigmoid, scale=0.0625)
            st["sg", c] = sg

        def scale2(c, eng=nc.vector):
            yb = kt([P, C, 4], BF16, "yb%d" % c)
            eng.tensor_tensor(
                out=yb[:], in0=st["sg", c][:], in1=gt_t[:].unsqueeze(1).to_broadcast([P, C, 4]), op=MULT,
            )
            st["yb", c] = yb[:].rearrange("p n t -> p (n t)")

        def mm3(c):
            w, s = st["ybq", c]
            b = psum.tile([P, 4, C], F32, name="b3_%d" % c, tag="bank", bufs=8)
            product(lambda t: b[:, t, :], w2w, w2s, FP4X4, 2 * P, w[:], s[:], C)
            st["b3", c] = b

        def evac3(c, vec=False):
            of = kt([P, 4, C], F32, "of%d" % c)
            if vec:
                nc.vector.tensor_copy(out=of[:], in_=st["b3", c][:])
            else:
                nc.scalar.copy(out=of[:], in_=st["b3", c][:])
            st["of", c] = of

        def store0(c, eng=nc.sync):
            eng.dma_start(out=out0_v[:, :, c * C : (c + 1) * C], in_=st["of", c][:])

        def weave3(c, vec=False):
            ob = kt([P, C, 4], BF16, "ob%d" % c)
            if vec:
                nc.vector.tensor_copy(
                    out=ob[:].rearrange("p (c i) t -> p c t i", i=4), in_=st["of", c][:].rearrange("p t (c i) -> p c t i", i=4)
                )
            else:
                nc.scalar.copy(out=ob[:], in_=st["b3", c][:].rearrange("p t n -> p n t"))
            st["ob", c] = ob[:].rearrange("p n t -> p (n t)")

        def quant3(c):
            nc.vector.quantize_mx(out=ow[:, c * C : (c + 1) * C].bitcast(FP8X4), scales=osc[:, c * C : (c + 1) * C], in_=st["ob", c])

        def store1(a, b, eng=nc.sync):
            eng.dma_start(out=out1_v[:, a * C : b * C], in_=ow[:, a * C : b * C])

        def store2(engs):
            for q in range(4):
                engs[q].dma_start(out=out_2[0, 4 * q : 4 * q + 4, :].bitcast(I32), in_=osc[32 * q : 32 * q + 4, :].bitcast(I32))

        deal_words(nc.vector, w1w, w1w_raw)
        gather_qs_all()
        deal_bytes(nc.vector, w1s, w1s_raw)
        gather_qw(0)
        mm1h(0)
        gather_qw(1)
        mm1h(1)
        gather_cs()
        gather_cw()
        weave1(0)
        weave1(1)
        quant("zb", 0)
        mm2(0)
        sigm(0)
        quant("zb", 1)
        mm2(1)
        sigm(1)
        weave1(2)
        weave1(3)
        quant("zb", 2)
        mm2(2)
        sigm(2)
        quant("zb", 3)
        mm2(3)
        sigm(3)
        deal_words(nc.vector, w2w, w2w_raw)
        deal_bytes(nc.vector, w2s, w2s_raw)
        scale2(0)
        scale2(1)
        quant("yb", 0)
        mm3(0)
        evac3(0)
        store0(0)
        scale2(2)
        quant("yb", 1)
        mm3(1)
        evac3(1)
        store0(1)
        scale2(3)
        quant("yb", 2)
        mm3(2)
        evac3(2)
        store0(2)
        quant("yb", 3)
        mm3(3)
        evac3(3)
        store0(3)
        weave3(0, True)
        weave3(1, True)
        quant3(0)
        quant3(1)
        store1(0, 2)
        weave3(2, True)
        quant3(2)
        weave3(3, True)
        quant3(3)
        store1(2, 4)
        store2([nc.sync, nc.scalar, nc.scalar, nc.scalar])
